import numpy as np
import ml_dtypes


def mxq(x, axis, fmt="e4m3"):
    dtype, down = {"e4m3": (ml_dtypes.float8_e4m3fn, 7), "e5m2": (ml_dtypes.float8_e5m2, 14)}[fmt]
    v = np.moveaxis(np.asarray(x, np.float32).astype(ml_dtypes.bfloat16).astype(np.float64), axis, -1)
    blocks = v.reshape(v.shape[:-1] + (-1, 32))
    amax = np.abs(blocks).max(-1, keepdims=True)
    byte = np.maximum(np.where(amax > 0, np.frexp(amax)[1] - 1 + 127, 0) - down, 1)
    scale = np.exp2(byte - 127.0)
    codes = (blocks / scale).astype(np.float32).astype(dtype).astype(np.float64)
    return np.moveaxis((codes * scale).reshape(v.shape), -1, axis)


WIDE = False


def mx_kscale(k):
    if not WIDE:
        return np.ones(k)
    levels = np.array([10, -10, 5, -5, 0])
    if k % 512:
        return np.exp2(np.random.permutation(np.resize(levels, k // 32))).repeat(32)
    a = np.empty((k // 512, 16))
    for p in range(k // 512):
        a[p, :8] = np.random.permutation(np.resize(levels, 8))
        for g in range(8):
            far = levels[np.abs(levels - a[p, g]) >= 10]
            a[p, g + 8] = far[np.random.randint(len(far))]
    return np.exp2(a.ravel()).repeat(32)


def f64(x):
    return np.asarray(x).astype(np.float64)


def striped8(idx):
    return np.asarray(idx).reshape(8, -1, 16).transpose(0, 2, 1).reshape(128, -1).astype(np.uint16)


def unstriped8(offs):
    return offs.reshape(8, 16, -1).transpose(0, 2, 1).reshape(8, -1).astype(np.int64)


def pick8(x, idx, run):
    r = np.arange(len(x))
    return x[r[:, None], idx[r % (8 * run) // run]]


E2M1 = np.array([0.0, 0.5, 1.0, 1.5, 2.0, 3.0, 4.0, 6.0, -0.0, -0.5, -1.0, -1.5, -2.0, -3.0, -4.0, -6.0])


def pack_weight(w, fmt):
    k, n = w.shape
    w = f64(np.asarray(w, np.float32).astype(ml_dtypes.bfloat16)).reshape(k // 32, 32, n)
    amax = np.abs(w).max(1)
    if fmt == "e4m3":
        byte = np.frexp(amax)[1] - 1 + 127 - 7
    else:
        mant, ex = np.frexp(amax / 6.0)
        byte = np.where(mant > 0.5, ex, ex - 1) + 127
    byte = np.clip(np.where(amax > 0, byte, 1), 1, 254)
    scaled = (w * np.exp2(127.0 - byte)[:, None, :]).reshape(k, n).astype(np.float32)
    by_word = np.ascontiguousarray(scaled.reshape(k // 512, 128, 4, n).transpose(0, 1, 3, 2))
    if fmt == "e4m3":
        words = by_word.astype(ml_dtypes.float8_e4m3fn).view(np.uint8)
    else:
        c = by_word.astype(ml_dtypes.float4_e2m1fn).view(np.uint8) & 0xF
        words = (c[..., 0::2] | (c[..., 1::2] << 4)).reshape(k // 512, 128, 2 * n)
    return np.ascontiguousarray(words), np.ascontiguousarray(byte.astype(np.uint8).reshape(k // 512, 16, n))


def unpack_weight(words, scales, fmt):
    g, _, n = scales.shape
    words = np.ascontiguousarray(words).reshape(g, 128, n, -1)
    if fmt == "e4m3":
        vals = words.view(ml_dtypes.float8_e4m3fn).astype(np.float64)
    else:
        nib = np.empty((g, 128, n, 4), np.uint8)
        nib[..., 0::2] = words & 0xF
        nib[..., 1::2] = words >> 4
        vals = E2M1[nib]
    vals = vals * np.repeat(np.exp2(scales.astype(np.float64) - 127.0), 8, axis=1)[..., None]
    return vals.transpose(0, 1, 3, 2).reshape(g * 512, n)


D, K, T, U, I, Q = 512, 512, 1024, 1024, 512, 128


def setup_inputs():
    n = np.random.standard_normal
    idx = np.stack([np.random.permutation(T)[:I] for _ in range(8)])
    idx2 = np.stack([np.random.permutation(U)[:I] for _ in range(8)])
    idx3 = np.stack([np.random.permutation(U)[:I] for _ in range(8)])
    idx4 = np.stack([np.random.permutation(U)[:I] for _ in range(8)])
    idx5 = np.stack([np.random.permutation(T)[:I] for _ in range(8)])
    idx6 = np.stack([np.random.permutation(T)[:I] for _ in range(8)])
    fd = mx_kscale(D)
    fk = mx_kscale(K)
    wqp = pack_weight(n((D, K)) * 1.0 / np.sqrt(D) * fd[:, None] * fk, "e4m3")
    cachep = pack_weight(n((K, T)) * 1.0 / np.sqrt(K) / fk[:, None], "e2m1")
    draftp = pack_weight(n((D, U)) * 1.0 / np.sqrt(D) * fd[:, None], "e4m3")
    return {
        "states": (n((D, Q)) * 0.95 / fd[:, None]).astype(np.float32),
        "wq_words": wqp[0],
        "wq_scales": wqp[1],
        "cache_words": cachep[0],
        "cache_scales": cachep[1],
        "draft_words": draftp[0],
        "draft_scales": draftp[1],
        "offs": striped8(idx),
        "offs2": striped8(idx2),
        "offs3": striped8(idx3),
        "offs4": striped8(idx4),
        "offs5": striped8(idx5),
        "offs6": striped8(idx6),
    }


def reference(states, wq_words, wq_scales, cache_words, cache_scales, draft_words, draft_scales, offs, offs2, offs3, offs4, offs5, offs6):
    idx = unstriped8(offs)
    idx2 = unstriped8(offs2)
    idx3 = unstriped8(offs3)
    idx4 = unstriped8(offs4)
    idx5 = unstriped8(offs5)
    idx6 = unstriped8(offs6)
    wqu = unpack_weight(wq_words, wq_scales, "e4m3")
    cacheu = unpack_weight(cache_words, cache_scales, "e2m1")
    draftu = unpack_weight(draft_words, draft_scales, "e4m3")
    statesq = mxq(f64(states), 0, "e4m3")
    qv = wqu.T @ statesq
    qvq = mxq(qv, 0, "e4m3")
    a = qvq.T @ cacheu
    b = statesq.T @ draftu
    f1 = np.zeros((Q, U))
    f1[np.arange(Q)[:, None], idx2[np.arange(Q) % 128 // 16]] = pick8(a, idx, 16)
    bb = b + f1
    w = np.maximum(pick8(bb, idx3, 16), pick8(bb, idx4, 16))
    f2 = np.zeros((Q, T))
    f2[np.arange(Q)[:, None], idx5[np.arange(Q) % 128 // 16]] = w
    aa = a - f2
    y = pick8(aa, idx6, 16)
    return y

@@ -1,0 +1,154 @@
+from contextlib import ExitStack
+
+import concourse.mybir as mybir
+
+F32 = mybir.dt.float32
+BF16 = mybir.dt.bfloat16
+I32 = mybir.dt.int32
+U16 = mybir.dt.uint16
+U8 = mybir.dt.uint8
+FP8X4 = mybir.dt.float8_e4m3fn_x4
+FP4X4 = mybir.dt.float4_e2m1fn_x4
+COPY = mybir.ActivationFunctionType.Copy
+ADD = mybir.AluOpType.add
+SUBTRACT = mybir.AluOpType.subtract
+MAX = mybir.AluOpType.max
+
+D, K, T, U, SLOTS, Q = 512, 512, 1024, 1024, 512, 128
+P = 128
+PACK = 4
+BANK = 512
+A_PIECE = 256
+HALF = SLOTS // 2
+LIST_COLS = SLOTS // 16
+FLOPS = 2 * (D * K * Q + K * Q * T + D * Q * U)
+
+
+def tile_attend_doubleread_side_kernel(tc, states, wq_words, wq_scales, cache_words, cache_scales, draft_words,
+                                        draft_scales, offs, offs2, offs3, offs4, offs5, offs6, out):
+    nc = tc.nc
+    with ExitStack() as ctx:
+        sb = ctx.enter_context(tc.tile_pool(name="sb", bufs=1))
+        ps = ctx.enter_context(tc.psum_pool(name="ps", bufs=1))
+
+        def half_of(lst, h):
+            return lst[:, h * (LIST_COLS // 2):(h + 1) * (LIST_COLS // 2)]
+
+        wq_plane_raw = sb.tile([P, K], U8, name="wq_plane_raw", align_bytes=64)
+        cache_plane = sb.tile([P, T], U8, name="cache_plane", align_bytes=64)
+        draft_plane = sb.tile([P, U], U8, name="draft_plane", align_bytes=64)
+        f1 = sb.tile([P, U], F32, name="f1", align_bytes=64)
+        f2 = sb.tile([P, T], F32, name="f2", align_bytes=64)
+        nc.vector.memset(cache_plane[:].bitcast(I32), 0)
+        nc.vector.memset(wq_plane_raw[:].bitcast(I32), 0)
+        nc.vector.memset(draft_plane[:].bitcast(I32), 0)
+        nc.vector.memset(f1[:], 0.0)
+        nc.vector.memset(f2[:], 0.0)
+
+        wq_rows = sb.tile([4, 4, K // 4], I32, name="wq_rows", align_bytes=64)
+        nc.sync.dma_start(wq_rows[:], wq_scales[0].bitcast(I32).rearrange("(g j) c -> j g c", j=4))
+        states_raw = sb.tile([P, PACK, Q], F32, name="states_raw", align_bytes=256)
+        nc.sync.dma_start(states_raw[:], states.rearrange("(p j) q -> p j q", j=PACK))
+        wq_raw = sb.tile([P, K], I32, name="wq_raw", align_bytes=256)
+        nc.sync.dma_start(wq_raw[:], wq_words[0].rearrange("p n t -> p (n t)").bitcast(I32))
+        cache_w = sb.tile([P, 2 * T], U8, name="cache_w", align_bytes=256)
+        nc.sync.dma_start(cache_w[:].bitcast(I32), cache_words[0].bitcast(I32))
+
+        def load_plane(plane, rows):
+            for g in range(4):
+                nc.sync.dma_start(plane[32 * g:32 * g + 4, :].bitcast(I32), rows[4 * g:4 * g + 4, :].bitcast(I32))
+
+        def load_list(src, name):
+            lst = sb.tile([P, LIST_COLS], U16, name=name)
+            nc.sync.dma_start(lst[:], src)
+            return lst
+
+        load_plane(cache_plane, cache_scales[0])
+        list1 = load_list(offs, "list1")
+        list2 = load_list(offs2, "list2")
+        draft_w = sb.tile([P, U], I32, name="draft_w", align_bytes=256)
+        nc.sync.dma_start(draft_w[:], draft_words[0].rearrange("p n t -> p (n t)").bitcast(I32))
+        load_plane(draft_plane, draft_scales[0])
+        list3 = load_list(offs3, "list3")
+        list4 = load_list(offs4, "list4")
+        list5 = load_list(offs5, "list5")
+        list6 = load_list(offs6, "list6")
+
+        for g in range(4):
+            nc.vector.tensor_copy(wq_plane_raw[32 * g:32 * g + 4, :].bitcast(I32), wq_rows[:, g, :])
+        wq_plane = sb.tile([P, PACK, P], U8, name="wq_plane", align_bytes=64)
+        nc.vector.tensor_copy(wq_plane[:].rearrange("p t m -> p m t"),
+                              wq_plane_raw[:].rearrange("p (m t) -> p m t", t=PACK))
+
+        states_bf = sb.tile([P, Q, PACK], BF16, name="states_bf", align_bytes=64)
+        nc.scalar.activation(states_bf[:, Q // 2:, :], states_raw[:, :, Q // 2:].rearrange("p j q -> p q j"), COPY)
+        nc.vector.tensor_copy(states_bf[:, :Q // 2, :], states_raw[:, :, :Q // 2].rearrange("p j q -> p q j"))
+        states_w = sb.tile([P, Q], I32, name="states_w", align_bytes=64)
+        states_plane = sb.tile([P, Q], U8, name="states_plane", align_bytes=64)
+        nc.vector.quantize_mx(states_w[:].bitcast(FP8X4), states_plane[:], states_bf[:].rearrange("p q j -> p (q j)"))
+
+        wq_w = sb.tile([P, PACK, P], I32, name="wq_w", align_bytes=64)
+        nc.vector.tensor_copy(wq_w[:].rearrange("p t m -> p m t"), wq_raw[:].rearrange("p (m t) -> p m t", t=PACK))
+
+        qv_ps = ps.tile([P, PACK, Q], F32, name="qv_ps")
+        for t in range(PACK):
+            nc.tensor.matmul_mx(qv_ps[:, t, :], lhsT=wq_w[:, t, :].bitcast(FP8X4), lhsT_scale=wq_plane[:, t, :],
+                                rhs=states_w[:].bitcast(FP8X4), rhs_scale=states_plane[:], start=True, stop=True)
+        qv_bf = sb.tile([P, Q, PACK], BF16, name="qv_bf", align_bytes=64)
+        nc.scalar.activation(qv_bf[:], qv_ps[:].rearrange("p t q -> p q t"), COPY)
+        qv_w = sb.tile([P, Q], I32, name="qv_w", align_bytes=64)
+        qv_plane = sb.tile([P, Q], U8, name="qv_plane", align_bytes=64)
+        nc.vector.quantize_mx(qv_w[:].bitcast(FP8X4), qv_plane[:], qv_bf[:].rearrange("p q j -> p (q j)"))
+
+        a = sb.tile([P, T], F32, name="a", align_bytes=64)
+        for n in range(T // A_PIECE):
+            cols = slice(n * A_PIECE, (n + 1) * A_PIECE)
+            a_ps = ps.tile([P, A_PIECE], F32, name="a_ps%d" % n)
+            nc.tensor.matmul_mx(a_ps[:], lhsT=qv_w[:].bitcast(FP8X4), lhsT_scale=qv_plane[:],
+                                rhs=cache_w[:, 2 * cols.start:2 * cols.stop].bitcast(FP4X4),
+                                rhs_scale=cache_plane[:, cols], start=True, stop=True)
+            if n % 2 == 0:
+                nc.scalar.activation(a[:, cols], a_ps[:], COPY)
+            else:
+                nc.vector.tensor_copy(a[:, cols], a_ps[:])
+
+        b_banks = []
+        for n in range(U // BANK):
+            cols = slice(n * BANK, (n + 1) * BANK)
+            b_ps = ps.tile([P, BANK], F32, name="b_ps%d" % n)
+            nc.tensor.matmul_mx(b_ps[:], lhsT=states_w[:].bitcast(FP8X4), lhsT_scale=states_plane[:],
+                                rhs=draft_w[:, cols].bitcast(FP8X4), rhs_scale=draft_plane[:, cols],
+                                start=True, stop=True)
+            b_banks.append(b_ps)
+
+        for h in range(2):
+            picked = sb.tile([P, HALF], F32, name="picked%d" % h, align_bytes=64)
+            nc.vector.tensor_copy(picked[:], a[:].indirect(half_of(list1, h)))
+            nc.scalar.activation(f1[:].indirect(half_of(list2, h)), picked[:], COPY)
+
+        bb = sb.tile([P, U], F32, name="bb", align_bytes=64)
+        for n in range(U // BANK):
+            cols = slice(n * BANK, (n + 1) * BANK)
+            nc.vector.tensor_tensor(bb[:, cols], b_banks[n][:], f1[:, cols], ADD)
+
+        left = sb.tile([P, HALF], F32, name="left", align_bytes=64)
+        right = sb.tile([P, HALF], F32, name="right", align_bytes=64)
+        for h in range(2):
+            w = sb.tile([P, HALF], F32, name="w%d" % h, align_bytes=64)
+            nc.vector.tensor_copy(left[:], bb[:].indirect(half_of(list3, h)))
+            if h == 0:
+                nc.scalar.activation(right[:], bb[:].indirect(half_of(list4, h)), COPY)
+            else:
+                nc.vector.tensor_copy(right[:], bb[:].indirect(half_of(list4, h)))
+            nc.vector.tensor_tensor(w[:], left[:], right[:], MAX)
+            nc.scalar.activation(f2[:].indirect(half_of(list5, h)), w[:], COPY)
+
+        aa = sb.tile([P, T], F32, name="aa", align_bytes=64)
+        nc.vector.tensor_tensor(aa[:], a[:], f2[:], SUBTRACT)
+
+        y0 = sb.tile([P, HALF], F32, name="y0", align_bytes=64)
+        y1 = sb.tile([P, HALF], F32, name="y1", align_bytes=64)
+        nc.vector.tensor_copy(y0[:], aa[:].indirect(half_of(list6, 0)))
+        nc.sync.dma_start(out[:, :HALF], y0[:])
+        nc.scalar.activation(y1[:], aa[:].indirect(half_of(list6, 1)), COPY)
+        nc.scalar.dma_start(out[:, HALF:], y1[:])

@@ -5,6 +5,7 @@ import concourse.mybir as mybir
 F32 = mybir.dt.float32
 BF16 = mybir.dt.bfloat16
 I32 = mybir.dt.int32
+U32 = mybir.dt.uint32
 U16 = mybir.dt.uint16
 U8 = mybir.dt.uint8
 FP8X4 = mybir.dt.float8_e4m3fn_x4
@@ -18,7 +19,9 @@ D, K, T, U, SLOTS, Q = 512, 512, 1024, 1024, 512, 128
 P = 128
 PACK = 4
 BANK = 512
-A_PIECE = 256
+A_EDGES = (0, 256, 512, 768, 896, 1024)
+DEAL_SPLIT = 96
+LEAD = 64
 HALF = SLOTS // 2
 LIST_COLS = SLOTS // 16
 FLOPS = 2 * (D * K * Q + K * Q * T + D * Q * U)
@@ -38,62 +41,64 @@ def tile_attend_doubleread_side_kernel(tc, states, wq_words, wq_scales, cache_wo
         cache_plane = sb.tile([P, T], U8, name="cache_plane", align_bytes=64)
         draft_plane = sb.tile([P, U], U8, name="draft_plane", align_bytes=64)
         f1 = sb.tile([P, U], F32, name="f1", align_bytes=64)
-        f2 = sb.tile([P, T], F32, name="f2", align_bytes=64)
+        f2_last = sb.tile([P, T], F32, name="f2_last", align_bytes=64)
+        nc.gpsimd.memset(wq_plane_raw[:].bitcast(I32), 0)
         nc.vector.memset(cache_plane[:].bitcast(I32), 0)
-        nc.vector.memset(wq_plane_raw[:].bitcast(I32), 0)
         nc.vector.memset(draft_plane[:].bitcast(I32), 0)
         nc.vector.memset(f1[:], 0.0)
-        nc.vector.memset(f2[:], 0.0)
+        nc.vector.memset(f2_last[:], 0.0)
 
-        wq_rows = sb.tile([4, 4, K // 4], I32, name="wq_rows", align_bytes=64)
-        nc.sync.dma_start(wq_rows[:], wq_scales[0].bitcast(I32).rearrange("(g j) c -> j g c", j=4))
-        states_raw = sb.tile([P, PACK, Q], F32, name="states_raw", align_bytes=256)
-        nc.sync.dma_start(states_raw[:], states.rearrange("(p j) q -> p j q", j=PACK))
-        wq_raw = sb.tile([P, K], I32, name="wq_raw", align_bytes=256)
-        nc.sync.dma_start(wq_raw[:], wq_words[0].rearrange("p n t -> p (n t)").bitcast(I32))
-        cache_w = sb.tile([P, 2 * T], U8, name="cache_w", align_bytes=256)
-        nc.sync.dma_start(cache_w[:].bitcast(I32), cache_words[0].bitcast(I32))
-
-        def load_plane(plane, rows):
-            for g in range(4):
-                nc.sync.dma_start(plane[32 * g:32 * g + 4, :].bitcast(I32), rows[4 * g:4 * g + 4, :].bitcast(I32))
+        def load_plane(plane, scales, queues):
+            for g, queue in enumerate(queues):
+                queue.dma_start(plane[32 * g:32 * g + 4, :].bitcast(I32), scales[0, 4 * g:4 * g + 4, :].bitcast(I32))
 
         def load_list(src, name):
             lst = sb.tile([P, LIST_COLS], U16, name=name)
             nc.sync.dma_start(lst[:], src)
             return lst
 
-        load_plane(cache_plane, cache_scales[0])
+        states_raw = sb.tile([P, PACK, Q], F32, name="states_raw", align_bytes=256)
+        nc.sync.dma_start(states_raw[:], states.rearrange("(p j) q -> p j q", j=PACK))
+        load_plane(wq_plane_raw, wq_scales, (nc.scalar, nc.scalar, nc.sync, nc.sync))
+        wq_raw = sb.tile([P, K], I32, name="wq_raw", tag="wq_raw", align_bytes=256)
+        nc.sync.dma_start(wq_raw[:], wq_words[0].rearrange("p n t -> p (n t)").bitcast(I32))
+        cache_w = sb.tile([P, 2 * T], U8, name="cache_w", align_bytes=256)
+        nc.sync.dma_start(cache_w[:].bitcast(I32), cache_words[0].bitcast(I32))
+        load_plane(cache_plane, cache_scales, [nc.sync] * 4)
         list1 = load_list(offs, "list1")
         list2 = load_list(offs2, "list2")
         draft_w = sb.tile([P, U], I32, name="draft_w", align_bytes=256)
         nc.sync.dma_start(draft_w[:], draft_words[0].rearrange("p n t -> p (n t)").bitcast(I32))
-        load_plane(draft_plane, draft_scales[0])
+        load_plane(draft_plane, draft_scales, [nc.sync] * 4)
         list3 = load_list(offs3, "list3")
         list4 = load_list(offs4, "list4")
         list5 = load_list(offs5, "list5")
         list6 = load_list(offs6, "list6")
 
-        for g in range(4):
-            nc.vector.tensor_copy(wq_plane_raw[32 * g:32 * g + 4, :].bitcast(I32), wq_rows[:, g, :])
+        states_bf = sb.tile([P, Q, PACK], BF16, name="states_bf", align_bytes=64)
+        nc.scalar.activation(states_bf[:, Q // 2:, :], states_raw[:, :, Q // 2:].rearrange("p j q -> p q j"), COPY)
+        nc.vector.tensor_copy(states_bf[:, :Q // 2, :], states_raw[:, :, :Q // 2].rearrange("p j q -> p q j"))
         wq_plane = sb.tile([P, PACK, P], U8, name="wq_plane", align_bytes=64)
         nc.vector.tensor_copy(wq_plane[:].rearrange("p t m -> p m t"),
                               wq_plane_raw[:].rearrange("p (m t) -> p m t", t=PACK))
 
-        states_bf = sb.tile([P, Q, PACK], BF16, name="states_bf", align_bytes=64)
-        nc.scalar.activation(states_bf[:, Q // 2:, :], states_raw[:, :, Q // 2:].rearrange("p j q -> p q j"), COPY)
-        nc.vector.tensor_copy(states_bf[:, :Q // 2, :], states_raw[:, :, :Q // 2].rearrange("p j q -> p q j"))
         states_w = sb.tile([P, Q], I32, name="states_w", align_bytes=64)
         states_plane = sb.tile([P, Q], U8, name="states_plane", align_bytes=64)
         nc.vector.quantize_mx(states_w[:].bitcast(FP8X4), states_plane[:], states_bf[:].rearrange("p q j -> p (q j)"))
 
         wq_w = sb.tile([P, PACK, P], I32, name="wq_w", align_bytes=64)
-        nc.vector.tensor_copy(wq_w[:].rearrange("p t m -> p m t"), wq_raw[:].rearrange("p (m t) -> p m t", t=PACK))
+        dealt = wq_w[:].bitcast(U32).rearrange("p t m -> p m t")
+        undealt = wq_raw[:].bitcast(U32).rearrange("p (m t) -> p m t", t=PACK)
+        nc.scalar.copy(dealt[:, :DEAL_SPLIT, :], undealt[:, :DEAL_SPLIT, :])
+        nc.vector.tensor_copy(wq_w[:].rearrange("p t m -> p m t")[:, DEAL_SPLIT:, :],
+                              wq_raw[:].rearrange("p (m t) -> p m t", t=PACK)[:, DEAL_SPLIT:, :])
 
         qv_ps = ps.tile([P, PACK, Q], F32, name="qv_ps")
         for t in range(PACK):
             nc.tensor.matmul_mx(qv_ps[:, t, :], lhsT=wq_w[:, t, :].bitcast(FP8X4), lhsT_scale=wq_plane[:, t, :],
                                 rhs=states_w[:].bitcast(FP8X4), rhs_scale=states_plane[:], start=True, stop=True)
+        f2_first = sb.tile([P, T], F32, name="f2_first", tag="wq_raw", align_bytes=256)
+        nc.vector.memset(f2_first[:], 0.0)
         qv_bf = sb.tile([P, Q, PACK], BF16, name="qv_bf", align_bytes=64)
         nc.scalar.activation(qv_bf[:], qv_ps[:].rearrange("p t q -> p q t"), COPY)
         qv_w = sb.tile([P, Q], I32, name="qv_w", align_bytes=64)
@@ -101,9 +106,9 @@ def tile_attend_doubleread_side_kernel(tc, states, wq_words, wq_scales, cache_wo
         nc.vector.quantize_mx(qv_w[:].bitcast(FP8X4), qv_plane[:], qv_bf[:].rearrange("p q j -> p (q j)"))
 
         a = sb.tile([P, T], F32, name="a", align_bytes=64)
-        for n in range(T // A_PIECE):
-            cols = slice(n * A_PIECE, (n + 1) * A_PIECE)
-            a_ps = ps.tile([P, A_PIECE], F32, name="a_ps%d" % n)
+        for n in range(len(A_EDGES) - 1):
+            cols = slice(A_EDGES[n], A_EDGES[n + 1])
+            a_ps = ps.tile([P, cols.stop - cols.start], F32, name="a_ps%d" % n, tag="bank%d" % n)
             nc.tensor.matmul_mx(a_ps[:], lhsT=qv_w[:].bitcast(FP8X4), lhsT_scale=qv_plane[:],
                                 rhs=cache_w[:, 2 * cols.start:2 * cols.stop].bitcast(FP4X4),
                                 rhs_scale=cache_plane[:, cols], start=True, stop=True)
@@ -112,39 +117,41 @@ def tile_attend_doubleread_side_kernel(tc, states, wq_words, wq_scales, cache_wo
             else:
                 nc.vector.tensor_copy(a[:, cols], a_ps[:])
 
+        picked = sb.tile([P, SLOTS], F32, name="picked", align_bytes=64)
+        nc.vector.tensor_copy(picked[:, :HALF], a[:].indirect(half_of(list1, 0)))
+        nc.scalar.activation(picked[:, HALF:], a[:].indirect(half_of(list1, 1)), COPY)
+        nc.scalar.activation(f1[:].indirect(list2[:]), picked[:], COPY)
+
         b_banks = []
         for n in range(U // BANK):
             cols = slice(n * BANK, (n + 1) * BANK)
-            b_ps = ps.tile([P, BANK], F32, name="b_ps%d" % n)
+            b_ps = ps.tile([P, BANK], F32, name="b_ps%d" % n, tag="bank%d" % n)
             nc.tensor.matmul_mx(b_ps[:], lhsT=states_w[:].bitcast(FP8X4), lhsT_scale=states_plane[:],
                                 rhs=draft_w[:, cols].bitcast(FP8X4), rhs_scale=draft_plane[:, cols],
                                 start=True, stop=True)
             b_banks.append(b_ps)
-
-        for h in range(2):
-            picked = sb.tile([P, HALF], F32, name="picked%d" % h, align_bytes=64)
-            nc.vector.tensor_copy(picked[:], a[:].indirect(half_of(list1, h)))
-            nc.scalar.activation(f1[:].indirect(half_of(list2, h)), picked[:], COPY)
 
         bb = sb.tile([P, U], F32, name="bb", align_bytes=64)
         for n in range(U // BANK):
             cols = slice(n * BANK, (n + 1) * BANK)
             nc.vector.tensor_tensor(bb[:, cols], b_banks[n][:], f1[:, cols], ADD)
 
-        left = sb.tile([P, HALF], F32, name="left", align_bytes=64)
+        left = sb.tile([P, SLOTS], F32, name="left", align_bytes=64)
         right = sb.tile([P, HALF], F32, name="right", align_bytes=64)
+        w = sb.tile([P, SLOTS], F32, name="w", align_bytes=64)
+        nc.scalar.activation(right[:], bb[:].indirect(half_of(list4, 0)), COPY)
         for h in range(2):
-            w = sb.tile([P, HALF], F32, name="w%d" % h, align_bytes=64)
-            nc.vector.tensor_copy(left[:], bb[:].indirect(half_of(list3, h)))
-            if h == 0:
-                nc.scalar.activation(right[:], bb[:].indirect(half_of(list4, h)), COPY)
-            else:
-                nc.vector.tensor_copy(right[:], bb[:].indirect(half_of(list4, h)))
-            nc.vector.tensor_tensor(w[:], left[:], right[:], MAX)
-            nc.scalar.activation(f2[:].indirect(half_of(list5, h)), w[:], COPY)
+            nc.vector.tensor_copy(left[:, h * HALF:(h + 1) * HALF], bb[:].indirect(half_of(list3, h)))
+        for start, stop, window in ((0, LEAD, f2_last), (LEAD, HALF, f2_first), (HALF, SLOTS, f2_last)):
+            if start == HALF:
+                nc.vector.tensor_copy(right[:], bb[:].indirect(half_of(list4, 1)))
+            nc.vector.tensor_tensor(w[:, start:stop], left[:, start:stop], right[:, start % HALF:(stop - 1) % HALF + 1], MAX)
+            nc.scalar.activation(window[:].indirect(list5[:, start // 16:stop // 16]), w[:, start:stop], COPY)
 
         aa = sb.tile([P, T], F32, name="aa", align_bytes=64)
-        nc.vector.tensor_tensor(aa[:], a[:], f2[:], SUBTRACT)
+        a_part = sb.tile([P, T], F32, name="a_part", align_bytes=64)
+        nc.vector.tensor_tensor(a_part[:], a[:], f2_first[:], SUBTRACT)
+        nc.vector.tensor_tensor(aa[:], a_part[:], f2_last[:], SUBTRACT)
 
         y0 = sb.tile([P, HALF], F32, name="y0", align_bytes=64)
         y1 = sb.tile([P, HALF], F32, name="y1", align_bytes=64)

@@ -22,6 +22,7 @@ BANK = 512
 A_EDGES = (0, 256, 512, 768, 896, 1024)
 DEAL_SPLIT = 96
 LEAD = 64
+ADD_SPLIT = 256
 HALF = SLOTS // 2
 LIST_COLS = SLOTS // 16
 FLOPS = 2 * (D * K * Q + K * Q * T + D * Q * U)
@@ -62,10 +63,10 @@ def tile_attend_doubleread_side_kernel(tc, states, wq_words, wq_scales, cache_wo
         load_plane(wq_plane_raw, wq_scales, (nc.scalar, nc.scalar, nc.sync, nc.sync))
         wq_raw = sb.tile([P, K], I32, name="wq_raw", tag="wq_raw", align_bytes=256)
         nc.sync.dma_start(wq_raw[:], wq_words[0].rearrange("p n t -> p (n t)").bitcast(I32))
+        list1 = load_list(offs, "list1")
         cache_w = sb.tile([P, 2 * T], U8, name="cache_w", align_bytes=256)
         nc.sync.dma_start(cache_w[:].bitcast(I32), cache_words[0].bitcast(I32))
         load_plane(cache_plane, cache_scales, [nc.sync] * 4)
-        list1 = load_list(offs, "list1")
         list2 = load_list(offs2, "list2")
         draft_w = sb.tile([P, U], I32, name="draft_w", align_bytes=256)
         nc.sync.dma_start(draft_w[:], draft_words[0].rearrange("p n t -> p (n t)").bitcast(I32))
@@ -131,10 +132,12 @@ def tile_attend_doubleread_side_kernel(tc, states, wq_words, wq_scales, cache_wo
                                 start=True, stop=True)
             b_banks.append(b_ps)
 
+        b_head = sb.tile([P, ADD_SPLIT], F32, name="b_head", align_bytes=64)
+        nc.vector.tensor_copy(b_head[:], b_banks[0][:, :ADD_SPLIT])
         bb = sb.tile([P, U], F32, name="bb", align_bytes=64)
-        for n in range(U // BANK):
-            cols = slice(n * BANK, (n + 1) * BANK)
-            nc.vector.tensor_tensor(bb[:, cols], b_banks[n][:], f1[:, cols], ADD)
+        nc.gpsimd.tensor_tensor(bb[:, :ADD_SPLIT], b_head[:], f1[:, :ADD_SPLIT], ADD)
+        nc.vector.tensor_tensor(bb[:, ADD_SPLIT:BANK], b_banks[0][:, ADD_SPLIT:], f1[:, ADD_SPLIT:BANK], ADD)
+        nc.vector.tensor_tensor(bb[:, BANK:], b_banks[1][:], f1[:, BANK:], ADD)
 
         left = sb.tile([P, SLOTS], F32, name="left", align_bytes=64)
         right = sb.tile([P, HALF], F32, name="right", align_bytes=64)

@@ -94,14 +94,16 @@ def tile_attend_doubleread_side_kernel(tc, states, wq_words, wq_scales, cache_wo
         nc.vector.tensor_copy(wq_w[:].rearrange("p t m -> p m t")[:, DEAL_SPLIT:, :],
                               wq_raw[:].rearrange("p (m t) -> p m t", t=PACK)[:, DEAL_SPLIT:, :])
 
-        qv_ps = ps.tile([P, PACK, Q], F32, name="qv_ps")
+        qv_banks = [ps.tile([P, 2, Q], F32, name="qv_ps%d" % u) for u in range(2)]
         for t in range(PACK):
-            nc.tensor.matmul_mx(qv_ps[:, t, :], lhsT=wq_w[:, t, :].bitcast(FP8X4), lhsT_scale=wq_plane[:, t, :],
-                                rhs=states_w[:].bitcast(FP8X4), rhs_scale=states_plane[:], start=True, stop=True)
+            nc.tensor.matmul_mx(qv_banks[t // 2][:, t % 2, :], lhsT=wq_w[:, t, :].bitcast(FP8X4),
+                                lhsT_scale=wq_plane[:, t, :], rhs=states_w[:].bitcast(FP8X4),
+                                rhs_scale=states_plane[:], start=True, stop=True)
         f2_first = sb.tile([P, T], F32, name="f2_first", tag="wq_raw", align_bytes=256)
         nc.vector.memset(f2_first[:], 0.0)
         qv_bf = sb.tile([P, Q, PACK], BF16, name="qv_bf", align_bytes=64)
-        nc.scalar.activation(qv_bf[:], qv_ps[:].rearrange("p t q -> p q t"), COPY)
+        nc.vector.tensor_copy(qv_bf[:, :, 0:2], qv_banks[0][:].rearrange("p t q -> p q t"))
+        nc.scalar.activation(qv_bf[:, :, 2:4], qv_banks[1][:].rearrange("p t q -> p q t"), COPY)
         qv_w = sb.tile([P, Q], I32, name="qv_w", align_bytes=64)
         qv_plane = sb.tile([P, Q], U8, name="qv_plane", align_bytes=64)
         nc.vector.quantize_mx(qv_w[:].bitcast(FP8X4), qv_plane[:], qv_bf[:].rearrange("p q j -> p (q j)"))

from contextlib import ExitStack

import concourse.mybir as mybir

F32 = mybir.dt.float32
BF16 = mybir.dt.bfloat16
I32 = mybir.dt.int32
U32 = mybir.dt.uint32
U16 = mybir.dt.uint16
U8 = mybir.dt.uint8
FP8X4 = mybir.dt.float8_e4m3fn_x4
FP4X4 = mybir.dt.float4_e2m1fn_x4
COPY = mybir.ActivationFunctionType.Copy
ADD = mybir.AluOpType.add
SUBTRACT = mybir.AluOpType.subtract
MAX = mybir.AluOpType.max

D, K, T, U, SLOTS, Q = 512, 512, 1024, 1024, 512, 128
P = 128
PACK = 4
BANK = 512
A_EDGES = (0, 256, 512, 768, 896, 1024)
DEAL_SPLIT = 96
LEAD = 64
ADD_SPLIT = 256
HALF = SLOTS // 2
LIST_COLS = SLOTS // 16
FLOPS = 2 * (D * K * Q + K * Q * T + D * Q * U)


def tile_attend_doubleread_side_kernel(tc, states, wq_words, wq_scales, cache_words, cache_scales, draft_words,
                                        draft_scales, offs, offs2, offs3, offs4, offs5, offs6, out):
    nc = tc.nc
    with ExitStack() as ctx:
        sb = ctx.enter_context(tc.tile_pool(name="sb", bufs=1))
        ps = ctx.enter_context(tc.psum_pool(name="ps", bufs=1))

        def half_of(lst, h):
            return lst[:, h * (LIST_COLS // 2):(h + 1) * (LIST_COLS // 2)]

        wq_plane_raw = sb.tile([P, K], U8, name="wq_plane_raw", align_bytes=64)
        cache_plane = sb.tile([P, T], U8, name="cache_plane", align_bytes=64)
        draft_plane = sb.tile([P, U], U8, name="draft_plane", align_bytes=64)
        f1 = sb.tile([P, U], F32, name="f1", align_bytes=64)
        f2_last = sb.tile([P, T], F32, name="f2_last", align_bytes=64)
        nc.gpsimd.memset(wq_plane_raw[:].bitcast(I32), 0)
        nc.vector.memset(cache_plane[:].bitcast(I32), 0)
        nc.vector.memset(draft_plane[:].bitcast(I32), 0)
        nc.vector.memset(f1[:], 0.0)
        nc.vector.memset(f2_last[:], 0.0)

        def load_plane(plane, scales, queues):
            for g, queue in enumerate(queues):
                queue.dma_start(plane[32 * g:32 * g + 4, :].bitcast(I32), scales[0, 4 * g:4 * g + 4, :].bitcast(I32))

        def load_list(src, name):
            lst = sb.tile([P, LIST_COLS], U16, name=name)
            nc.sync.dma_start(lst[:], src)
            return lst

        states_raw = sb.tile([P, PACK, Q], F32, name="states_raw", align_bytes=256)
        nc.sync.dma_start(states_raw[:], states.rearrange("(p j) q -> p j q", j=PACK))
        load_plane(wq_plane_raw, wq_scales, (nc.scalar, nc.scalar, nc.sync, nc.sync))
        wq_raw = sb.tile([P, K], I32, name="wq_raw", tag="wq_raw", align_bytes=256)
        nc.sync.dma_start(wq_raw[:], wq_words[0].rearrange("p n t -> p (n t)").bitcast(I32))
        list1 = load_list(offs, "list1")
        cache_w = sb.tile([P, 2 * T], U8, name="cache_w", align_bytes=256)
        nc.sync.dma_start(cache_w[:].bitcast(I32), cache_words[0].bitcast(I32))
        load_plane(cache_plane, cache_scales, [nc.sync] * 4)
        list2 = load_list(offs2, "list2")
        draft_w = sb.tile([P, U], I32, name="draft_w", align_bytes=256)
        nc.sync.dma_start(draft_w[:], draft_words[0].rearrange("p n t -> p (n t)").bitcast(I32))
        load_plane(draft_plane, draft_scales, [nc.sync] * 4)
        list3 = load_list(offs3, "list3")
        list4 = load_list(offs4, "list4")
        list5 = load_list(offs5, "list5")
        list6 = load_list(offs6, "list6")

        states_bf = sb.tile([P, Q, PACK], BF16, name="states_bf", align_bytes=64)
        nc.scalar.activation(states_bf[:, Q // 2:, :], states_raw[:, :, Q // 2:].rearrange("p j q -> p q j"), COPY)
        nc.vector.tensor_copy(states_bf[:, :Q // 2, :], states_raw[:, :, :Q // 2].rearrange("p j q -> p q j"))
        wq_plane = sb.tile([P, PACK, P], U8, name="wq_plane", align_bytes=64)
        nc.vector.tensor_copy(wq_plane[:].rearrange("p t m -> p m t"),
                              wq_plane_raw[:].rearrange("p (m t) -> p m t", t=PACK))

        states_w = sb.tile([P, Q], I32, name="states_w", align_bytes=64)
        states_plane = sb.tile([P, Q], U8, name="states_plane", align_bytes=64)
        nc.vector.quantize_mx(states_w[:].bitcast(FP8X4), states_plane[:], states_bf[:].rearrange("p q j -> p (q j)"))

        wq_w = sb.tile([P, PACK, P], I32, name="wq_w", align_bytes=64)
        dealt = wq_w[:].bitcast(U32).rearrange("p t m -> p m t")
        undealt = wq_raw[:].bitcast(U32).rearrange("p (m t) -> p m t", t=PACK)
        nc.scalar.copy(dealt[:, :DEAL_SPLIT, :], undealt[:, :DEAL_SPLIT, :])
        nc.vector.tensor_copy(wq_w[:].rearrange("p t m -> p m t")[:, DEAL_SPLIT:, :],
                              wq_raw[:].rearrange("p (m t) -> p m t", t=PACK)[:, DEAL_SPLIT:, :])

        qv_banks = [ps.tile([P, 2, Q], F32, name="qv_ps%d" % u) for u in range(2)]
        for t in range(PACK):
            nc.tensor.matmul_mx(qv_banks[t // 2][:, t % 2, :], lhsT=wq_w[:, t, :].bitcast(FP8X4),
                                lhsT_scale=wq_plane[:, t, :], rhs=states_w[:].bitcast(FP8X4),
                                rhs_scale=states_plane[:], start=True, stop=True)
        f2_first = sb.tile([P, T], F32, name="f2_first", tag="wq_raw", align_bytes=256)
        nc.vector.memset(f2_first[:], 0.0)
        qv_bf = sb.tile([P, Q, PACK], BF16, name="qv_bf", align_bytes=64)
        nc.vector.tensor_copy(qv_bf[:, :, 0:2], qv_banks[0][:].rearrange("p t q -> p q t"))
        nc.scalar.activation(qv_bf[:, :, 2:4], qv_banks[1][:].rearrange("p t q -> p q t"), COPY)
        qv_w = sb.tile([P, Q], I32, name="qv_w", align_bytes=64)
        qv_plane = sb.tile([P, Q], U8, name="qv_plane", align_bytes=64)
        nc.vector.quantize_mx(qv_w[:].bitcast(FP8X4), qv_plane[:], qv_bf[:].rearrange("p q j -> p (q j)"))

        a = sb.tile([P, T], F32, name="a", align_bytes=64)
        for n in range(len(A_EDGES) - 1):
            cols = slice(A_EDGES[n], A_EDGES[n + 1])
            a_ps = ps.tile([P, cols.stop - cols.start], F32, name="a_ps%d" % n, tag="bank%d" % n)
            nc.tensor.matmul_mx(a_ps[:], lhsT=qv_w[:].bitcast(FP8X4), lhsT_scale=qv_plane[:],
                                rhs=cache_w[:, 2 * cols.start:2 * cols.stop].bitcast(FP4X4),
                                rhs_scale=cache_plane[:, cols], start=True, stop=True)
            if n % 2 == 0:
                nc.scalar.activation(a[:, cols], a_ps[:], COPY)
            else:
                nc.vector.tensor_copy(a[:, cols], a_ps[:])

        picked = sb.tile([P, SLOTS], F32, name="picked", align_bytes=64)
        nc.vector.tensor_copy(picked[:, :HALF], a[:].indirect(half_of(list1, 0)))
        nc.scalar.activation(picked[:, HALF:], a[:].indirect(half_of(list1, 1)), COPY)
        nc.scalar.activation(f1[:].indirect(list2[:]), picked[:], COPY)

        b_banks = []
        for n in range(U // BANK):
            cols = slice(n * BANK, (n + 1) * BANK)
            b_ps = ps.tile([P, BANK], F32, name="b_ps%d" % n, tag="bank%d" % n)
            nc.tensor.matmul_mx(b_ps[:], lhsT=states_w[:].bitcast(FP8X4), lhsT_scale=states_plane[:],
                                rhs=draft_w[:, cols].bitcast(FP8X4), rhs_scale=draft_plane[:, cols],
                                start=True, stop=True)
            b_banks.append(b_ps)

        b_head = sb.tile([P, ADD_SPLIT], F32, name="b_head", align_bytes=64)
        nc.vector.tensor_copy(b_head[:], b_banks[0][:, :ADD_SPLIT])
        bb = sb.tile([P, U], F32, name="bb", align_bytes=64)
        nc.gpsimd.tensor_tensor(bb[:, :ADD_SPLIT], b_head[:], f1[:, :ADD_SPLIT], ADD)
        nc.vector.tensor_tensor(bb[:, ADD_SPLIT:BANK], b_banks[0][:, ADD_SPLIT:], f1[:, ADD_SPLIT:BANK], ADD)
        nc.vector.tensor_tensor(bb[:, BANK:], b_banks[1][:], f1[:, BANK:], ADD)

        left = sb.tile([P, SLOTS], F32, name="left", align_bytes=64)
        right = sb.tile([P, HALF], F32, name="right", align_bytes=64)
        w = sb.tile([P, SLOTS], F32, name="w", align_bytes=64)
        nc.scalar.activation(right[:], bb[:].indirect(half_of(list4, 0)), COPY)
        for h in range(2):
            nc.vector.tensor_copy(left[:, h * HALF:(h + 1) * HALF], bb[:].indirect(half_of(list3, h)))
        for start, stop, window in ((0, LEAD, f2_last), (LEAD, HALF, f2_first), (HALF, SLOTS, f2_last)):
            if start == HALF:
                nc.vector.tensor_copy(right[:], bb[:].indirect(half_of(list4, 1)))
            nc.vector.tensor_tensor(w[:, start:stop], left[:, start:stop], right[:, start % HALF:(stop - 1) % HALF + 1], MAX)
            nc.scalar.activation(window[:].indirect(list5[:, start // 16:stop // 16]), w[:, start:stop], COPY)

        aa = sb.tile([P, T], F32, name="aa", align_bytes=64)
        a_part = sb.tile([P, T], F32, name="a_part", align_bytes=64)
        nc.vector.tensor_tensor(a_part[:], a[:], f2_first[:], SUBTRACT)
        nc.vector.tensor_tensor(aa[:], a_part[:], f2_last[:], SUBTRACT)

        y0 = sb.tile([P, HALF], F32, name="y0", align_bytes=64)
        y1 = sb.tile([P, HALF], F32, name="y1", align_bytes=64)
        nc.vector.tensor_copy(y0[:], aa[:].indirect(half_of(list6, 0)))
        nc.sync.dma_start(out[:, :HALF], y0[:])
        nc.scalar.activation(y1[:], aa[:].indirect(half_of(list6, 1)), COPY)
        nc.scalar.dma_start(out[:, HALF:], y1[:])
